import numpy as np
import ml_dtypes


def mxq(x, axis, fmt="e4m3"):
    dtype, down = {"e4m3": (ml_dtypes.float8_e4m3fn, 7), "e5m2": (ml_dtypes.float8_e5m2, 14)}[fmt]
    v = np.moveaxis(np.asarray(x, np.float32).astype(ml_dtypes.bfloat16).astype(np.float64), axis, -1)
    blocks = v.reshape(v.shape[:-1] + (-1, 32))
    amax = np.abs(blocks).max(-1, keepdims=True)
    byte = np.maximum(np.where(amax > 0, np.frexp(amax)[1] - 1 + 127, 0) - down, 1)
    scale = np.exp2(byte - 127.0)
    codes = (blocks / scale).astype(np.float32).astype(dtype).astype(np.float64)
    return np.moveaxis((codes * scale).reshape(v.shape), -1, axis)


WIDE = False


def mx_kscale(k):
    if not WIDE:
        return np.ones(k)
    levels = np.array([10, -10, 5, -5, 0])
    if k % 512:
        return np.exp2(np.random.permutation(np.resize(levels, k // 32))).repeat(32)
    a = np.empty((k // 512, 16))
    for p in range(k // 512):
        a[p, :8] = np.random.permutation(np.resize(levels, 8))
        for g in range(8):
            far = levels[np.abs(levels - a[p, g]) >= 10]
            a[p, g + 8] = far[np.random.randint(len(far))]
    return np.exp2(a.ravel()).repeat(32)


def f64(x):
    return np.asarray(x).astype(np.float64)


def striped(idx):
    return np.tile(idx.reshape(-1, 16).T, (8, 1)).astype(np.uint16)


def unstriped(offs):
    return offs[:16].T.reshape(-1).astype(np.int64)


def pack_weight(w):
    k, n = w.shape
    w = f64(np.asarray(w, np.float32).astype(ml_dtypes.bfloat16)).reshape(k // 32, 32, n)
    amax = np.abs(w).max(1)
    byte = np.clip(np.where(amax > 0, np.frexp(amax)[1] - 1 + 127 - 7, 1), 1, 254)
    scaled = (w * np.exp2(127.0 - byte)[:, None, :]).reshape(k, n).astype(np.float32)
    words = np.ascontiguousarray(scaled.reshape(k // 512, 128, 4, n).transpose(0, 1, 3, 2)).astype(ml_dtypes.float8_e4m3fn).view(np.uint8)
    return words, np.ascontiguousarray(byte.astype(np.uint8).reshape(k // 512, 16, n))


def unpack_weight(words, scales):
    g, p, n, _ = words.shape
    vals = np.ascontiguousarray(words).view(ml_dtypes.float8_e4m3fn).astype(np.float64) * np.repeat(np.exp2(scales.astype(np.float64) - 127.0), 8, axis=1)[..., None]
    return vals.transpose(0, 1, 3, 2).reshape(g * 512, n)

def planes(y):
    n, m = y.shape
    v = y.astype(np.float32).astype(ml_dtypes.bfloat16).astype(np.float64).reshape(n // 32, 32, m)
    top = np.abs(v).max(1)
    byte = np.clip(np.where(top > 0, np.frexp(top)[1] - 1 + 127 - 7, 1), 1, 254)
    codes = (v * np.exp2(127.0 - byte)[:, None, :]).reshape(n, m).astype(np.float32).astype(ml_dtypes.float8_e4m3fn).view(np.uint8)
    words = codes.reshape(n // 512, 128, 4, m).transpose(0, 1, 3, 2)
    return np.ascontiguousarray(words), np.ascontiguousarray(byte.astype(np.uint8).reshape(n // 512, 16, m))


K, T, N = 512, 512, 512
P = 2 ** 7


def setup_inputs():
    n = np.random.standard_normal
    s = mx_kscale(K)[:, None]
    packed_xT = pack_weight(n((K, T)) * s)
    return {
        "x_words": packed_xT[0],
        "x_scales": packed_xT[1],
        "w1": (n((K, N)) / np.sqrt(K) / s).astype(np.float32),
        "fx": np.tile(np.random.uniform(0.05, 0.95, T), (P, 1)).astype(np.float32),
        "fy": np.tile(np.random.uniform(0.05, 0.95, T), (P, 1)).astype(np.float32),
        "c00": striped(np.random.permutation(T)),
        "c01": striped(np.random.permutation(T)),
        "c10": striped(np.random.permutation(T)),
        "c11": striped(np.random.permutation(T)),
    }


def reference(x_words, x_scales, w1, fx, fy, c00, c01, c10, c11):
    xq = unpack_weight(x_words, x_scales)
    y = mxq(f64(w1), 0, "e4m3").T @ xq
    top = y[:, unstriped(c00)] + (y[:, unstriped(c01)] - y[:, unstriped(c00)]) * f64(fx)[:1]
    low = y[:, unstriped(c10)] + (y[:, unstriped(c11)] - y[:, unstriped(c10)]) * f64(fx)[:1]
    out_0 = top + (low - top) * f64(fy)[:1]
    return (out_0,) + planes(out_0)

@@ -1,0 +1,190 @@
+from contextlib import ExitStack
+
+import concourse.mybir as mybir
+from concourse.masks import make_identity
+
+K, T, N = 512, 512, 512
+FLOPS = 2 * K * T * N
+
+F32 = mybir.dt.float32
+BF16 = mybir.dt.bfloat16
+I32 = mybir.dt.int32
+U32 = mybir.dt.uint32
+U16 = mybir.dt.uint16
+U8 = mybir.dt.uint8
+FP8X4 = mybir.dt.float8_e4m3fn_x4
+MULT = mybir.AluOpType.mult
+ADD = mybir.AluOpType.add
+
+P = 128
+PACK = 4
+BLOCKS = 4
+SPARE = 16
+
+
+def tile_picked_wbilin_none_lo_kernel(tc, x_words, x_scales, w1, fx, fy, c00, c01, c10, c11, out_0, out_1, out_2):
+    nc = tc.nc
+    with ExitStack() as ctx:
+        keep = ctx.enter_context(tc.tile_pool(name="keep", bufs=1))
+        ring = ctx.enter_context(tc.tile_pool(name="ring", bufs=4))
+        sums = ctx.enter_context(tc.psum_pool(name="sums", bufs=1))
+        auxp = ctx.enter_context(tc.psum_pool(name="aux", bufs=1))
+        aux = [auxp.tile([P, T], F32, name=f"aux{a}") for a in range(4)]
+
+        lists = [keep.tile([P, T // 16], U16, name=f"list{i}") for i in range(4)]
+        list_src = [c11, c10, c00, c01]
+        xw = keep.tile([P, T], U32, name="xw", align_bytes=64)
+        xs = keep.tile([P, T], U8, name="xs", align_bytes=64)
+        xs_in = keep.tile([P, T // 4], I32, name="xs_in")
+        w_first = keep.tile([P, PACK, P], F32, name="w_first")
+        w_raw = [w_first, w_first] + [keep.tile([P, PACK, P], F32, name=f"w_raw{b}") for b in range(2, BLOCKS)]
+        w_rows = w1.rearrange("(p j) m -> p j m", j=PACK)
+        ax = keep.tile([P, 2, PACK], F32, name="ax")
+        ay = keep.tile([P, 2, PACK], F32, name="ay")
+
+        nc.gpsimd.memset(xs[:].bitcast(I32), 0)
+        nc.sync.dma_start(w_raw[0][:], w_rows[:, :, 0:P])
+        nc.scalar.dma_start(ax[:, 1, :], fx[0].rearrange("(p j) -> p j", j=PACK))
+        nc.scalar.dma_start(ay[:, 1, :], fy[0].rearrange("(p j) -> p j", j=PACK))
+        for q in range(4):
+            nc.sync.dma_start(xs_in[32 * q : 32 * q + 4, :], x_scales[0, 4 * q : 4 * q + 4, :].bitcast(I32))
+        nc.sync.dma_start(xw[:].bitcast(I32), x_words[0].rearrange("p n r -> p (n r)").bitcast(I32))
+        nc.sync.dma_start(lists[0][:], list_src[0])
+        nc.sync.dma_start(lists[1][:], list_src[1])
+        nc.sync.dma_start(lists[2][:], list_src[2])
+        nc.sync.dma_start(lists[3][:], list_src[3])
+        for b in range(2, BLOCKS):
+            nc.sync.dma_start(w_raw[b][:], w_rows[:, :, b * P : (b + 1) * P])
+
+        ident = keep.tile([P, P], F32, name="ident")
+        make_identity(nc, ident[:])
+        y = [keep.tile([P, T + SPARE if b < 3 else T], F32, name=f"y{b}") for b in range(BLOCKS)]
+        for b in range(3):
+            nc.gpsimd.memset(y[b][:, T:], 0.0)
+
+        wt = keep.tile([P, 4, PACK], F32, name="wt")
+        nc.vector.tensor_tensor(wt[:, 0, :], ax[:, 1, :], ay[:, 1, :], MULT)
+        nc.vector.tensor_scalar(ax[:, 0, :], ax[:, 1, :], -1.0, 1.0, MULT, ADD)
+        nc.vector.tensor_scalar(ay[:, 0, :], ay[:, 1, :], -1.0, 1.0, MULT, ADD)
+        nc.vector.tensor_tensor(wt[:, 1, :], ax[:, 0, :], ay[:, 1, :], MULT)
+        nc.vector.tensor_tensor(wt[:, 2:4, :], ax[:], ay[:, 0:1, :].to_broadcast([P, 2, PACK]), MULT)
+        cw = [keep.tile([P, T], F32, name=f"cw{i}") for i in range(4)]
+
+        acc = [sums.tile([P, N], F32, name=f"acc{h}") for h in range(BLOCKS)]
+
+        def spread(i, copy, bank):
+            for j in range(PACK):
+                nc.tensor.transpose(bank[:, j * P : (j + 1) * P], wt[:, i, j : j + 1].to_broadcast([P, P]), ident[:])
+            copy(cw[i][:].rearrange("q (n j) -> q n j", j=PACK), bank[:].rearrange("q (j n) -> q n j", j=PACK))
+
+        w_bf = [keep.tile([P, P, PACK], BF16, name="w_bf", align_bytes=64)] * BLOCKS
+        w_codes = [keep.tile([P, P], U32, name=f"w_codes{b}", align_bytes=64) for b in range(BLOCKS)]
+        w_sc = [keep.tile([P, P], U8, name=f"w_sc{b}", align_bytes=64) for b in range(BLOCKS)]
+
+        def cast(b, copy, lo, hi):
+            copy(
+                w_bf[b][:, lo:hi, :].rearrange("p (c i) j -> p c j i", i=4),
+                w_raw[b][:, :, lo:hi].rearrange("p j (c i) -> p c j i", i=4),
+            )
+            if hi == P and b == 0:
+                nc.sync.dma_start(w_raw[1][:], w_rows[:, :, P : 2 * P])
+
+        def quant_w(b):
+            nc.vector.quantize_mx(out=w_codes[b][:].bitcast(FP8X4), scales=w_sc[b][:], in_=w_bf[b][:].rearrange("p c j -> p (c j)"))
+
+        def project(b, lo, hi, copy, bank):
+            nc.tensor.matmul_mx(
+                out=bank[:, 0 : hi - lo], lhsT=w_codes[b][:].bitcast(FP8X4), lhsT_scale=w_sc[b][:],
+                rhs=xw[:, lo:hi].bitcast(FP8X4), rhs_scale=xs[:, lo:hi], start=True, stop=True,
+            )
+            copy(y[b][:, lo:hi], bank[:, 0 : hi - lo])
+
+        st = [keep.tile([P, PACK, P], F32, name=f"st{h}") for h in range(BLOCKS)]
+
+        def gather(b, i, h0, h1, window):
+            n = (h1 - h0) * P
+            g = ring.tile([P, n], F32, name=f"g{n}", bufs=8 if n == P else 4)[:]
+            nc.vector.tensor_tensor(g, window.indirect(lists[i][:, h0 * 8 : h1 * 8]), cw[i][:, h0 * P : h1 * P], MULT)
+            for h in range(h0, h1):
+                nc.tensor.matmul(
+                    acc[h][:, b * P : (b + 1) * P], lhsT=g[:, (h - h0) * P : (h - h0 + 1) * P], rhs=ident[:],
+                    is_transpose=True, start=(i == 0), stop=(i == 3),
+                )
+
+        def drain(b, h):
+            nc.scalar.copy(st[h][:, :, 32 * b : 32 * b + 32], acc[h][:, b * P : (b + 1) * P].rearrange("v (q t) -> v t q", t=PACK))
+
+        def turn_back(h, bank):
+            for t in range(PACK):
+                nc.tensor.transpose(bank[:, t * P : (t + 1) * P], st[h][:, t, :], ident[:])
+            return bank
+
+        words = keep.tile([P, T], U32, name="words", align_bytes=64)
+        scales = keep.tile([P, T], U8, name="scales", align_bytes=64)
+        out_rows = out_0.rearrange("(p t) v -> p t v", t=PACK)
+        out_words = out_1[0].rearrange("p n r -> p (n r)").bitcast(I32)
+
+        def store_f32(h, bank):
+            o = keep.tile([P, PACK, P], F32, name=f"o{h}")
+            nc.scalar.copy(o[:], bank[:].rearrange("p (t v) -> p t v", t=PACK))
+            nc.sync.dma_start(out_rows[:, :, h * P : (h + 1) * P], o[:])
+
+        r = keep.tile([P, T * PACK], BF16, name="r", align_bytes=64)
+
+        def round_bf16(h, bank, copy):
+            copy(r[:, h * T : (h + 1) * T].rearrange("p (v t) -> p v t", t=PACK), bank[:].rearrange("p (t v) -> p v t", t=PACK))
+
+        def quant_out(h0, h1):
+            cols = slice(h0 * P, h1 * P)
+            nc.vector.quantize_mx(out=words[:, cols].bitcast(FP8X4), scales=scales[:, cols], in_=r[:, h0 * T : h1 * T])
+            nc.sync.dma_start(out_words[:, cols], words[:, cols].bitcast(I32))
+
+        cast(0, nc.vector.tensor_copy, 0, 64)
+        cast(0, nc.scalar.copy, 64, P)
+        for q in range(4):
+            nc.vector.tensor_copy(xs[32 * q : 32 * q + 4, :].bitcast(I32), xs_in[32 * q : 32 * q + 4, :])
+        quant_w(0)
+        spread(0, nc.vector.tensor_copy, aux[2])
+        project(0, 0, 256, nc.vector.tensor_copy, aux[0])
+        project(0, 256, T, nc.scalar.copy, aux[1])
+        spread(1, nc.scalar.copy, aux[3])
+        cast(1, nc.scalar.copy, 0, P)
+        spread(2, nc.scalar.copy, aux[0])
+        spread(3, nc.scalar.copy, aux[1])
+
+        def corners(b, h0, h1, first=0):
+            for i in range(first, 4):
+                gather(b, i, h0, h1, y[b][:])
+            for h in range(h0, h1):
+                drain(b, h)
+
+        gather(0, 0, 0, BLOCKS, y[0][:])
+        for b in range(1, BLOCKS):
+            quant_w(b)
+            project(b, 0, T, nc.scalar.copy, aux[3 - b % 2])
+            if b < 3:
+                cast(b + 1, nc.scalar.copy, 0, P)
+        corners(0, 0, BLOCKS, 1)
+        corners(1, 0, BLOCKS)
+        corners(2, 0, BLOCKS)
+        corners(3, 0, 2)
+        turn_back(0, aux[0])
+        turn_back(1, aux[1])
+        corners(3, 2, 3)
+        turn_back(2, aux[2])
+        corners(3, 3, 4)
+        turn_back(3, aux[3])
+        turn_back(3, acc[0])
+        round_bf16(0, aux[0], nc.scalar.copy)
+        store_f32(0, aux[0])
+        round_bf16(1, aux[1], nc.vector.tensor_copy)
+        store_f32(1, aux[1])
+        quant_out(0, 2)
+        round_bf16(2, aux[2], nc.vector.tensor_copy)
+        store_f32(2, aux[2])
+        round_bf16(3, aux[3], nc.vector.tensor_copy)
+        store_f32(3, acc[0])
+        quant_out(2, 4)
+        for q in range(4):
+            eng = nc.sync if q < 2 else nc.scalar
+            eng.dma_start(out_2[0, 4 * q : 4 * q + 4, :].bitcast(I32), scales[32 * q : 32 * q + 4, :].bitcast(I32))

@@ -20,13 +20,15 @@ P = 128
 PACK = 4
 BLOCKS = 4
 SPARE = 16
+PIECES = [(0, 44), (44, 88), (88, 128)]
+PIECE_AT = [352, 0, 704]
+DRAINS = [(0, 42), (42, 85), (85, 128)]
 
 
 def tile_picked_wbilin_none_lo_kernel(tc, x_words, x_scales, w1, fx, fy, c00, c01, c10, c11, out_0, out_1, out_2):
     nc = tc.nc
     with ExitStack() as ctx:
         keep = ctx.enter_context(tc.tile_pool(name="keep", bufs=1))
-        ring = ctx.enter_context(tc.tile_pool(name="ring", bufs=4))
         sums = ctx.enter_context(tc.psum_pool(name="sums", bufs=1))
         auxp = ctx.enter_context(tc.psum_pool(name="aux", bufs=1))
         aux = [auxp.tile([P, T], F32, name=f"aux{a}") for a in range(4)]
@@ -36,31 +38,36 @@ def tile_picked_wbilin_none_lo_kernel(tc, x_words, x_scales, w1, fx, fy, c00, c0
         xw = keep.tile([P, T], U32, name="xw", align_bytes=64)
         xs = keep.tile([P, T], U8, name="xs", align_bytes=64)
         xs_in = keep.tile([P, T // 4], I32, name="xs_in")
-        w_first = keep.tile([P, PACK, P], F32, name="w_first")
-        w_raw = [w_first, w_first] + [keep.tile([P, PACK, P], F32, name=f"w_raw{b}") for b in range(2, BLOCKS)]
+        w_stage = keep.tile([P, 1344], F32, name="w_stage")
+        w_raw = [
+            w_stage[:, at : at + 16 * (q1 - q0)].rearrange("p (j m) -> p j m", j=PACK)
+            for (q0, q1), at in zip(PIECES, PIECE_AT)
+        ]
         w_rows = w1.rearrange("(p j) m -> p j m", j=PACK)
         ax = keep.tile([P, 2, PACK], F32, name="ax")
         ay = keep.tile([P, 2, PACK], F32, name="ay")
 
+        def load_w(a):
+            q0, q1 = PIECES[a]
+            nc.sync.dma_start(w_raw[a], w_rows[:, :, 4 * q0 : 4 * q1])
+
         nc.gpsimd.memset(xs[:].bitcast(I32), 0)
-        nc.sync.dma_start(w_raw[0][:], w_rows[:, :, 0:P])
+        load_w(0)
         nc.scalar.dma_start(ax[:, 1, :], fx[0].rearrange("(p j) -> p j", j=PACK))
         nc.scalar.dma_start(ay[:, 1, :], fy[0].rearrange("(p j) -> p j", j=PACK))
         for q in range(4):
             nc.sync.dma_start(xs_in[32 * q : 32 * q + 4, :], x_scales[0, 4 * q : 4 * q + 4, :].bitcast(I32))
         nc.sync.dma_start(xw[:].bitcast(I32), x_words[0].rearrange("p n r -> p (n r)").bitcast(I32))
-        nc.sync.dma_start(lists[0][:], list_src[0])
-        nc.sync.dma_start(lists[1][:], list_src[1])
-        nc.sync.dma_start(lists[2][:], list_src[2])
-        nc.sync.dma_start(lists[3][:], list_src[3])
-        for b in range(2, BLOCKS):
-            nc.sync.dma_start(w_raw[b][:], w_rows[:, :, b * P : (b + 1) * P])
+        for i in range(4):
+            nc.sync.dma_start(lists[i][:], list_src[i])
 
         ident = keep.tile([P, P], F32, name="ident")
         make_identity(nc, ident[:])
-        y = [keep.tile([P, T + SPARE if b < 3 else T], F32, name=f"y{b}") for b in range(BLOCKS)]
-        for b in range(3):
-            nc.gpsimd.memset(y[b][:, T:], 0.0)
+        y = [keep.tile([P, T + SPARE if b == 0 else T], F32, name=f"y{b}") for b in range(BLOCKS)]
+        nc.gpsimd.memset(y[0][:, T:], 0.0)
+        term_tiles = [keep.tile([P, T + P if i == 3 else T], F32, name=f"term{i}") for i in range(4)]
+        nc.gpsimd.memset(term_tiles[3][:, 0:P], 0.0)
+        term = [term_tiles[i][:, P:] if i == 3 else term_tiles[i][:] for i in range(4)]
 
         wt = keep.tile([P, 4, PACK], F32, name="wt")
         nc.vector.tensor_tensor(wt[:, 0, :], ax[:, 1, :], ay[:, 1, :], MULT)
@@ -69,7 +76,6 @@ def tile_picked_wbilin_none_lo_kernel(tc, x_words, x_scales, w1, fx, fy, c00, c0
         nc.vector.tensor_tensor(wt[:, 1, :], ax[:, 0, :], ay[:, 1, :], MULT)
         nc.vector.tensor_tensor(wt[:, 2:4, :], ax[:], ay[:, 0:1, :].to_broadcast([P, 2, PACK]), MULT)
         cw = [keep.tile([P, T], F32, name=f"cw{i}") for i in range(4)]
-
         acc = [sums.tile([P, N], F32, name=f"acc{h}") for h in range(BLOCKS)]
 
         def spread(i, copy, bank):
@@ -77,20 +83,26 @@ def tile_picked_wbilin_none_lo_kernel(tc, x_words, x_scales, w1, fx, fy, c00, c0
                 nc.tensor.transpose(bank[:, j * P : (j + 1) * P], wt[:, i, j : j + 1].to_broadcast([P, P]), ident[:])
             copy(cw[i][:].rearrange("q (n j) -> q n j", j=PACK), bank[:].rearrange("q (j n) -> q n j", j=PACK))
 
-        w_bf = [keep.tile([P, P, PACK], BF16, name="w_bf", align_bytes=64)] * BLOCKS
+        w_bf = keep.tile([P, N * PACK], BF16, name="w_bf", align_bytes=64)
         w_codes = [keep.tile([P, P], U32, name=f"w_codes{b}", align_bytes=64) for b in range(BLOCKS)]
         w_sc = [keep.tile([P, P], U8, name=f"w_sc{b}", align_bytes=64) for b in range(BLOCKS)]
 
-        def cast(b, copy, lo, hi):
+        def cast_mixed(a, copy):
+            q0, q1 = PIECES[a]
             copy(
-                w_bf[b][:, lo:hi, :].rearrange("p (c i) j -> p c j i", i=4),
-                w_raw[b][:, :, lo:hi].rearrange("p j (c i) -> p c j i", i=4),
+                w_bf[:, 12 * q0 : 12 * q1].rearrange("p (q t j) -> p q j t", t=3, j=PACK),
+                w_raw[a].rearrange("p j (q t) -> p q j t", t=PACK)[:, :, :, 0:3],
             )
-            if hi == P and b == 0:
-                nc.sync.dma_start(w_raw[1][:], w_rows[:, :, P : 2 * P])
+
+        def cast_plane(a):
+            q0, q1 = PIECES[a]
+            nc.scalar.copy(
+                w_bf[:, 1536 + 4 * q0 : 1536 + 4 * q1].rearrange("p (q j) -> p q j", j=PACK),
+                w_raw[a].rearrange("p j (q t) -> p q j t", t=PACK)[:, :, :, 3],
+            )
 
         def quant_w(b):
-            nc.vector.quantize_mx(out=w_codes[b][:].bitcast(FP8X4), scales=w_sc[b][:], in_=w_bf[b][:].rearrange("p c j -> p (c j)"))
+            nc.vector.quantize_mx(out=w_codes[b][:].bitcast(FP8X4), scales=w_sc[b][:], in_=w_bf[:, b * T : (b + 1) * T])
 
         def project(b, lo, hi, copy, bank):
             nc.tensor.matmul_mx(
@@ -101,10 +113,13 @@ def tile_picked_wbilin_none_lo_kernel(tc, x_words, x_scales, w1, fx, fy, c00, c0
 
         st = [keep.tile([P, PACK, P], F32, name=f"st{h}") for h in range(BLOCKS)]
 
-        def gather(b, i, h0, h1, window):
+        def look_up(g, b, i, h0, h1):
+            nc.vector.tensor_tensor(g, y[b][:].indirect(lists[i][:, h0 * 8 : h1 * 8]), cw[i][:, h0 * P : h1 * P], MULT)
+
+        def gather(b, i, h0, h1):
             n = (h1 - h0) * P
-            g = ring.tile([P, n], F32, name=f"g{n}", bufs=8 if n == P else 4)[:]
-            nc.vector.tensor_tensor(g, window.indirect(lists[i][:, h0 * 8 : h1 * 8]), cw[i][:, h0 * P : h1 * P], MULT)
+            g = term[i][:, 0:n]
+            look_up(g, b, i, h0, h1)
             for h in range(h0, h1):
                 nc.tensor.matmul(
                     acc[h][:, b * P : (b + 1) * P], lhsT=g[:, (h - h0) * P : (h - h0 + 1) * P], rhs=ident[:],
@@ -112,35 +127,43 @@ def tile_picked_wbilin_none_lo_kernel(tc, x_words, x_scales, w1, fx, fy, c00, c0
                 )
 
         def drain(b, h):
-            nc.scalar.copy(st[h][:, :, 32 * b : 32 * b + 32], acc[h][:, b * P : (b + 1) * P].rearrange("v (q t) -> v t q", t=PACK))
+            if b < 3:
+                q0, q1 = DRAINS[b]
+                nc.scalar.copy(st[h][:, 0:3, q0:q1], acc[h][:, 3 * q0 : 3 * q1].rearrange("v (q t) -> v t q", t=3))
+            else:
+                nc.scalar.copy(st[h][:, 3, :], acc[h][:, 3 * P :])
 
-        def turn_back(h, bank):
-            for t in range(PACK):
+        def turn_back(h, bank, planes):
+            for t in range(planes):
                 nc.tensor.transpose(bank[:, t * P : (t + 1) * P], st[h][:, t, :], ident[:])
-            return bank
 
         words = keep.tile([P, T], U32, name="words", align_bytes=64)
         scales = keep.tile([P, T], U8, name="scales", align_bytes=64)
         out_rows = out_0.rearrange("(p t) v -> p t v", t=PACK)
         out_words = out_1[0].rearrange("p n r -> p (n r)").bitcast(I32)
+        o = [keep.tile([P, PACK, P], F32, name=f"o{h}") for h in range(BLOCKS)]
 
-        def store_f32(h, bank):
-            o = keep.tile([P, PACK, P], F32, name=f"o{h}")
-            nc.scalar.copy(o[:], bank[:].rearrange("p (t v) -> p t v", t=PACK))
-            nc.sync.dma_start(out_rows[:, :, h * P : (h + 1) * P], o[:])
+        def store_f32(h, bank, planes):
+            nc.scalar.copy(o[h][:, 0:planes, :], bank[:, 0 : planes * P].rearrange("p (t v) -> p t v", t=planes))
+            nc.sync.dma_start(out_rows[:, 0:planes, h * P : (h + 1) * P], o[h][:, 0:planes, :])
 
         r = keep.tile([P, T * PACK], BF16, name="r", align_bytes=64)
 
-        def round_bf16(h, bank, copy):
-            copy(r[:, h * T : (h + 1) * T].rearrange("p (v t) -> p v t", t=PACK), bank[:].rearrange("p (t v) -> p v t", t=PACK))
+        def rounded(h):
+            return r[:, h * T : (h + 1) * T].rearrange("p (v t) -> p v t", t=PACK)
+
+        def round_bf16(h, bank, planes):
+            nc.scalar.copy(rounded(h)[:, :, 0:planes], bank[:, 0 : planes * P].rearrange("p (t v) -> p v t", t=planes))
 
         def quant_out(h0, h1):
             cols = slice(h0 * P, h1 * P)
             nc.vector.quantize_mx(out=words[:, cols].bitcast(FP8X4), scales=scales[:, cols], in_=r[:, h0 * T : h1 * T])
             nc.sync.dma_start(out_words[:, cols], words[:, cols].bitcast(I32))
 
-        cast(0, nc.vector.tensor_copy, 0, 64)
-        cast(0, nc.scalar.copy, 64, P)
+        cast_mixed(0, nc.vector.tensor_copy)
+        cast_plane(0)
+        load_w(1)
+        load_w(2)
         for q in range(4):
             nc.vector.tensor_copy(xs[32 * q : 32 * q + 4, :].bitcast(I32), xs_in[32 * q : 32 * q + 4, :])
         quant_w(0)
@@ -148,42 +171,61 @@ def tile_picked_wbilin_none_lo_kernel(tc, x_words, x_scales, w1, fx, fy, c00, c0
         project(0, 0, 256, nc.vector.tensor_copy, aux[0])
         project(0, 256, T, nc.scalar.copy, aux[1])
         spread(1, nc.scalar.copy, aux[3])
-        cast(1, nc.scalar.copy, 0, P)
+        cast_mixed(1, nc.scalar.copy)
         spread(2, nc.scalar.copy, aux[0])
         spread(3, nc.scalar.copy, aux[1])
 
         def corners(b, h0, h1, first=0):
             for i in range(first, 4):
-                gather(b, i, h0, h1, y[b][:])
+                gather(b, i, h0, h1)
             for h in range(h0, h1):
                 drain(b, h)
 
-        gather(0, 0, 0, BLOCKS, y[0][:])
-        for b in range(1, BLOCKS):
-            quant_w(b)
-            project(b, 0, T, nc.scalar.copy, aux[3 - b % 2])
-            if b < 3:
-                cast(b + 1, nc.scalar.copy, 0, P)
+        gather(0, 0, 0, BLOCKS)
+        quant_w(1)
+        project(1, 0, T, nc.scalar.copy, aux[2])
+        cast_mixed(2, nc.scalar.copy)
+        quant_w(2)
+        project(2, 0, T, nc.scalar.copy, aux[3])
+        cast_plane(1)
+        cast_plane(2)
+        quant_w(3)
+        project(3, 0, T, nc.scalar.copy, aux[2])
         corners(0, 0, BLOCKS, 1)
-        corners(1, 0, BLOCKS)
-        corners(2, 0, BLOCKS)
+        corners(1, 0, 2)
+        corners(2, 0, 2)
         corners(3, 0, 2)
-        turn_back(0, aux[0])
-        turn_back(1, aux[1])
+        turn_back(0, aux[0], 4)
+        turn_back(1, aux[1], 4)
+        for h in range(2):
+            round_bf16(h, aux[h], 4)
+            store_f32(h, aux[h], 4)
+        corners(1, 2, 4)
+        corners(2, 2, 4)
+        turn_back(3, aux[2], 3)
         corners(3, 2, 3)
-        turn_back(2, aux[2])
-        corners(3, 3, 4)
-        turn_back(3, aux[3])
-        turn_back(3, acc[0])
-        round_bf16(0, aux[0], nc.scalar.copy)
-        store_f32(0, aux[0])
-        round_bf16(1, aux[1], nc.vector.tensor_copy)
-        store_f32(1, aux[1])
+        turn_back(2, aux[3], 4)
+        store_f32(3, aux[2], 3)
+        round_bf16(3, aux[2], 2)
+        round_bf16(2, aux[3], 4)
+        store_f32(2, aux[3], 4)
+
+        pair_sum = keep.tile([P, P], F32, name="pair_sum")
+        for i in range(3):
+            look_up(term[i][:, 0:P], 3, i, 3, 4)
+        nc.vector.tensor_tensor(pair_sum[:], term[0][:, 0:P], term[1][:, 0:P], ADD)
         quant_out(0, 2)
-        round_bf16(2, aux[2], nc.vector.tensor_copy)
-        store_f32(2, aux[2])
-        round_bf16(3, aux[3], nc.vector.tensor_copy)
-        store_f32(3, acc[0])
+        nc.vector.tensor_tensor(o[3][:, 3, :], pair_sum[:], term[2][:, 0:P], ADD)
+        look_up(term[3][:, 0:P], 3, 3, 3, 4)
+        nc.vector.tensor_tensor(
+            rounded(3)[:, :, 2:4],
+            o[3][:, 2:4, :].rearrange("p t v -> p v t"),
+            term_tiles[3][:, 0 : 2 * P].rearrange("p (t v) -> p v t", t=2),
+            ADD,
+        )
+        final = keep.tile([P, P], F32, name="final")
+        nc.vector.tensor_tensor(final[:], o[3][:, 3, :], term[3][:, 0:P], ADD)
+        nc.scalar.dma_start(out_rows[:, 3, 3 * P :], final[:])
         quant_out(2, 4)
         for q in range(4):
             eng = nc.sync if q < 2 else nc.scalar

@@ -1,7 +1,6 @@
 from contextlib import ExitStack
 
 import concourse.mybir as mybir
-from concourse.masks import make_identity
 
 K, T, N = 512, 512, 512
 FLOPS = 2 * K * T * N
@@ -51,10 +50,9 @@ def tile_picked_wbilin_none_lo_kernel(tc, x_words, x_scales, w1, fx, fy, c00, c0
             q0, q1 = PIECES[a]
             nc.sync.dma_start(w_raw[a], w_rows[:, :, 4 * q0 : 4 * q1])
 
-        nc.gpsimd.memset(xs[:].bitcast(I32), 0)
+        nc.sync.dma_start(ax[:, 1, :], fx[0].rearrange("(p j) -> p j", j=PACK))
+        nc.sync.dma_start(ay[:, 1, :], fy[0].rearrange("(p j) -> p j", j=PACK))
         load_w(0)
-        nc.scalar.dma_start(ax[:, 1, :], fx[0].rearrange("(p j) -> p j", j=PACK))
-        nc.scalar.dma_start(ay[:, 1, :], fy[0].rearrange("(p j) -> p j", j=PACK))
         for q in range(4):
             nc.sync.dma_start(xs_in[32 * q : 32 * q + 4, :], x_scales[0, 4 * q : 4 * q + 4, :].bitcast(I32))
         nc.sync.dma_start(xw[:].bitcast(I32), x_words[0].rearrange("p n r -> p (n r)").bitcast(I32))
@@ -62,25 +60,36 @@ def tile_picked_wbilin_none_lo_kernel(tc, x_words, x_scales, w1, fx, fy, c00, c0
             nc.sync.dma_start(lists[i][:], list_src[i])
 
         ident = keep.tile([P, P], F32, name="ident")
-        make_identity(nc, ident[:])
+        ones = keep.tile([P, 32], F32, name="ones")
+        column = keep.tile([P, 32], F32, name="column", align_bytes=64)
+        row = keep.tile([P, 32], F32, name="row", align_bytes=64)
+        nc.vector.memset(ones[:], 1.0)
+        nc.vector.memset(ident[:], 0.0)
+        nc.vector.tensor_tensor_scan(column[:], ones[:], ones[:], 0.0, MULT, ADD)
+        nc.vector.memset(xs[:].bitcast(I32), 0)
+        nc.vector.transpose(row[:], column[:])
+        for q in range(4):
+            rows = slice(32 * q, 32 * q + 32)
+            nc.vector.tensor_tensor(ident[rows, rows], column[rows, :], row[rows, :], mybir.AluOpType.is_equal)
         y = [keep.tile([P, T + SPARE if b == 0 else T], F32, name=f"y{b}") for b in range(BLOCKS)]
-        nc.gpsimd.memset(y[0][:, T:], 0.0)
+        nc.vector.memset(y[0][:, T:], 0.0)
         term_tiles = [keep.tile([P, T + P if i == 3 else T], F32, name=f"term{i}") for i in range(4)]
-        nc.gpsimd.memset(term_tiles[3][:, 0:P], 0.0)
+        nc.vector.memset(term_tiles[3][:, 0:P], 0.0)
         term = [term_tiles[i][:, P:] if i == 3 else term_tiles[i][:] for i in range(4)]
 
-        wt = keep.tile([P, 4, PACK], F32, name="wt")
-        nc.vector.tensor_tensor(wt[:, 0, :], ax[:, 1, :], ay[:, 1, :], MULT)
+        wt = [keep.tile([P, PACK], F32, name=f"wt{i}") for i in range(4)]
+        nc.vector.tensor_tensor(wt[0][:], ax[:, 1, :], ay[:, 1, :], MULT)
         nc.vector.tensor_scalar(ax[:, 0, :], ax[:, 1, :], -1.0, 1.0, MULT, ADD)
         nc.vector.tensor_scalar(ay[:, 0, :], ay[:, 1, :], -1.0, 1.0, MULT, ADD)
-        nc.vector.tensor_tensor(wt[:, 1, :], ax[:, 0, :], ay[:, 1, :], MULT)
-        nc.vector.tensor_tensor(wt[:, 2:4, :], ax[:], ay[:, 0:1, :].to_broadcast([P, 2, PACK]), MULT)
+        nc.vector.tensor_tensor(wt[1][:], ax[:, 0, :], ay[:, 1, :], MULT)
+        nc.vector.tensor_tensor(wt[2][:], ax[:, 0, :], ay[:, 0, :], MULT)
+        nc.vector.tensor_tensor(wt[3][:], ax[:, 1, :], ay[:, 0, :], MULT)
         cw = [keep.tile([P, T], F32, name=f"cw{i}") for i in range(4)]
         acc = [sums.tile([P, N], F32, name=f"acc{h}") for h in range(BLOCKS)]
 
         def spread(i, copy, bank):
             for j in range(PACK):
-                nc.tensor.transpose(bank[:, j * P : (j + 1) * P], wt[:, i, j : j + 1].to_broadcast([P, P]), ident[:])
+                nc.tensor.transpose(bank[:, j * P : (j + 1) * P], wt[i][:, j : j + 1].to_broadcast([P, P]), ident[:])
             copy(cw[i][:].rearrange("q (n j) -> q n j", j=PACK), bank[:].rearrange("q (j n) -> q n j", j=PACK))
 
         w_bf = keep.tile([P, N * PACK], BF16, name="w_bf", align_bytes=64)
@@ -94,9 +103,9 @@ def tile_picked_wbilin_none_lo_kernel(tc, x_words, x_scales, w1, fx, fy, c00, c0
                 w_raw[a].rearrange("p j (q t) -> p q j t", t=PACK)[:, :, :, 0:3],
             )
 
-        def cast_plane(a):
+        def cast_plane(a, copy):
             q0, q1 = PIECES[a]
-            nc.scalar.copy(
+            copy(
                 w_bf[:, 1536 + 4 * q0 : 1536 + 4 * q1].rearrange("p (q j) -> p q j", j=PACK),
                 w_raw[a].rearrange("p j (q t) -> p q j t", t=PACK)[:, :, :, 3],
             )
@@ -161,13 +170,13 @@ def tile_picked_wbilin_none_lo_kernel(tc, x_words, x_scales, w1, fx, fy, c00, c0
             nc.sync.dma_start(out_words[:, cols], words[:, cols].bitcast(I32))
 
         cast_mixed(0, nc.vector.tensor_copy)
-        cast_plane(0)
+        cast_plane(0, nc.vector.tensor_copy)
         load_w(1)
         load_w(2)
         for q in range(4):
             nc.vector.tensor_copy(xs[32 * q : 32 * q + 4, :].bitcast(I32), xs_in[32 * q : 32 * q + 4, :])
         quant_w(0)
-        spread(0, nc.vector.tensor_copy, aux[2])
+        spread(0, nc.scalar.copy, aux[2])
         project(0, 0, 256, nc.vector.tensor_copy, aux[0])
         project(0, 256, T, nc.scalar.copy, aux[1])
         spread(1, nc.scalar.copy, aux[3])
@@ -187,8 +196,8 @@ def tile_picked_wbilin_none_lo_kernel(tc, x_words, x_scales, w1, fx, fy, c00, c0
         cast_mixed(2, nc.scalar.copy)
         quant_w(2)
         project(2, 0, T, nc.scalar.copy, aux[3])
-        cast_plane(1)
-        cast_plane(2)
+        cast_plane(1, nc.scalar.copy)
+        cast_plane(2, nc.scalar.copy)
         quant_w(3)
         project(3, 0, T, nc.scalar.copy, aux[2])
         corners(0, 0, BLOCKS, 1)

@@ -73,9 +73,12 @@ def tile_picked_wbilin_none_lo_kernel(tc, x_words, x_scales, w1, fx, fy, c00, c0
             nc.vector.tensor_tensor(ident[rows, rows], column[rows, :], row[rows, :], mybir.AluOpType.is_equal)
         y = [keep.tile([P, T + SPARE if b == 0 else T], F32, name=f"y{b}") for b in range(BLOCKS)]
         nc.vector.memset(y[0][:, T:], 0.0)
-        term_tiles = [keep.tile([P, T + P if i == 3 else T], F32, name=f"term{i}") for i in range(4)]
-        nc.vector.memset(term_tiles[3][:, 0:P], 0.0)
-        term = [term_tiles[i][:, P:] if i == 3 else term_tiles[i][:] for i in range(4)]
+        w_words = keep.tile([P, 2 * N], F32, name="w_words", align_bytes=64)
+        term0 = keep.tile([P, T], F32, name="term0")
+        term1 = keep.tile([P, T], F32, name="term1")
+        term3 = keep.tile([P, P + T], F32, name="term3")
+        nc.vector.memset(term3[:, 0:P], 0.0)
+        term = [term0[:], term1[:], w_words[:, 0:T], term3[:, P:]]
 
         wt = [keep.tile([P, PACK], F32, name=f"wt{i}") for i in range(4)]
         nc.vector.tensor_tensor(wt[0][:], ax[:, 1, :], ay[:, 1, :], MULT)
@@ -92,7 +95,7 @@ def tile_picked_wbilin_none_lo_kernel(tc, x_words, x_scales, w1, fx, fy, c00, c0
                 nc.tensor.transpose(bank[:, j * P : (j + 1) * P], wt[i][:, j : j + 1].to_broadcast([P, P]), ident[:])
             copy(cw[i][:].rearrange("q (n j) -> q n j", j=PACK), bank[:].rearrange("q (j n) -> q n j", j=PACK))
 
-        w_bf = keep.tile([P, N * PACK], BF16, name="w_bf", align_bytes=64)
+        w_bf = w_words[:].bitcast(BF16)
         w_codes = [keep.tile([P, P], U32, name=f"w_codes{b}", align_bytes=64) for b in range(BLOCKS)]
         w_sc = [keep.tile([P, P], U8, name=f"w_sc{b}", align_bytes=64) for b in range(BLOCKS)]
 
@@ -103,9 +106,9 @@ def tile_picked_wbilin_none_lo_kernel(tc, x_words, x_scales, w1, fx, fy, c00, c0
                 w_raw[a].rearrange("p j (q t) -> p q j t", t=PACK)[:, :, :, 0:3],
             )
 
-        def cast_plane(a, copy):
+        def cast_plane(a):
             q0, q1 = PIECES[a]
-            copy(
+            nc.scalar.copy(
                 w_bf[:, 1536 + 4 * q0 : 1536 + 4 * q1].rearrange("p (q j) -> p q j", j=PACK),
                 w_raw[a].rearrange("p j (q t) -> p q j t", t=PACK)[:, :, :, 3],
             )
@@ -128,6 +131,8 @@ def tile_picked_wbilin_none_lo_kernel(tc, x_words, x_scales, w1, fx, fy, c00, c0
         def gather(b, i, h0, h1):
             n = (h1 - h0) * P
             g = term[i][:, 0:n]
+            if i == 0 and h0 == 0 and b in (1, 2):
+                g = w_words[:, (b + 1) * 256 : (b + 2) * 256]
             look_up(g, b, i, h0, h1)
             for h in range(h0, h1):
                 nc.tensor.matmul(
@@ -170,7 +175,7 @@ def tile_picked_wbilin_none_lo_kernel(tc, x_words, x_scales, w1, fx, fy, c00, c0
             nc.sync.dma_start(out_words[:, cols], words[:, cols].bitcast(I32))
 
         cast_mixed(0, nc.vector.tensor_copy)
-        cast_plane(0, nc.vector.tensor_copy)
+        cast_plane(0)
         load_w(1)
         load_w(2)
         for q in range(4):
@@ -196,8 +201,8 @@ def tile_picked_wbilin_none_lo_kernel(tc, x_words, x_scales, w1, fx, fy, c00, c0
         cast_mixed(2, nc.scalar.copy)
         quant_w(2)
         project(2, 0, T, nc.scalar.copy, aux[3])
-        cast_plane(1, nc.scalar.copy)
-        cast_plane(2, nc.scalar.copy)
+        cast_plane(1)
+        cast_plane(2)
         quant_w(3)
         project(3, 0, T, nc.scalar.copy, aux[2])
         corners(0, 0, BLOCKS, 1)
@@ -229,7 +234,7 @@ def tile_picked_wbilin_none_lo_kernel(tc, x_words, x_scales, w1, fx, fy, c00, c0
         nc.vector.tensor_tensor(
             rounded(3)[:, :, 2:4],
             o[3][:, 2:4, :].rearrange("p t v -> p v t"),
-            term_tiles[3][:, 0 : 2 * P].rearrange("p (t v) -> p v t", t=2),
+            term3[:, 0 : 2 * P].rearrange("p (t v) -> p v t", t=2),
             ADD,
         )
         final = keep.tile([P, P], F32, name="final")

@@ -36,7 +36,6 @@ def tile_picked_wbilin_none_lo_kernel(tc, x_words, x_scales, w1, fx, fy, c00, c0
         list_src = [c11, c10, c00, c01]
         xw = keep.tile([P, T], U32, name="xw", align_bytes=64)
         xs = keep.tile([P, T], U8, name="xs", align_bytes=64)
-        xs_in = keep.tile([P, T // 4], I32, name="xs_in")
         w_stage = keep.tile([P, 1344], F32, name="w_stage")
         w_raw = [
             w_stage[:, at : at + 16 * (q1 - q0)].rearrange("p (j m) -> p j m", j=PACK)
@@ -50,11 +49,12 @@ def tile_picked_wbilin_none_lo_kernel(tc, x_words, x_scales, w1, fx, fy, c00, c0
             q0, q1 = PIECES[a]
             nc.sync.dma_start(w_raw[a], w_rows[:, :, 4 * q0 : 4 * q1])
 
+        nc.vector.memset(xs[:].bitcast(I32), 0)
         nc.sync.dma_start(ax[:, 1, :], fx[0].rearrange("(p j) -> p j", j=PACK))
         nc.sync.dma_start(ay[:, 1, :], fy[0].rearrange("(p j) -> p j", j=PACK))
         load_w(0)
         for q in range(4):
-            nc.sync.dma_start(xs_in[32 * q : 32 * q + 4, :], x_scales[0, 4 * q : 4 * q + 4, :].bitcast(I32))
+            nc.sync.dma_start(xs[32 * q : 32 * q + 4, :].bitcast(I32), x_scales[0, 4 * q : 4 * q + 4, :].bitcast(I32))
         nc.sync.dma_start(xw[:].bitcast(I32), x_words[0].rearrange("p n r -> p (n r)").bitcast(I32))
         for i in range(4):
             nc.sync.dma_start(lists[i][:], list_src[i])
@@ -66,7 +66,6 @@ def tile_picked_wbilin_none_lo_kernel(tc, x_words, x_scales, w1, fx, fy, c00, c0
         nc.vector.memset(ones[:], 1.0)
         nc.vector.memset(ident[:], 0.0)
         nc.vector.tensor_tensor_scan(column[:], ones[:], ones[:], 0.0, MULT, ADD)
-        nc.vector.memset(xs[:].bitcast(I32), 0)
         nc.vector.transpose(row[:], column[:])
         for q in range(4):
             rows = slice(32 * q, 32 * q + 32)
@@ -106,9 +105,9 @@ def tile_picked_wbilin_none_lo_kernel(tc, x_words, x_scales, w1, fx, fy, c00, c0
                 w_raw[a].rearrange("p j (q t) -> p q j t", t=PACK)[:, :, :, 0:3],
             )
 
-        def cast_plane(a):
+        def cast_plane(a, copy):
             q0, q1 = PIECES[a]
-            nc.scalar.copy(
+            copy(
                 w_bf[:, 1536 + 4 * q0 : 1536 + 4 * q1].rearrange("p (q j) -> p q j", j=PACK),
                 w_raw[a].rearrange("p j (q t) -> p q j t", t=PACK)[:, :, :, 3],
             )
@@ -175,11 +174,9 @@ def tile_picked_wbilin_none_lo_kernel(tc, x_words, x_scales, w1, fx, fy, c00, c0
             nc.sync.dma_start(out_words[:, cols], words[:, cols].bitcast(I32))
 
         cast_mixed(0, nc.vector.tensor_copy)
-        cast_plane(0)
+        cast_plane(0, nc.vector.tensor_copy)
         load_w(1)
         load_w(2)
-        for q in range(4):
-            nc.vector.tensor_copy(xs[32 * q : 32 * q + 4, :].bitcast(I32), xs_in[32 * q : 32 * q + 4, :])
         quant_w(0)
         spread(0, nc.scalar.copy, aux[2])
         project(0, 0, 256, nc.vector.tensor_copy, aux[0])
@@ -201,8 +198,8 @@ def tile_picked_wbilin_none_lo_kernel(tc, x_words, x_scales, w1, fx, fy, c00, c0
         cast_mixed(2, nc.scalar.copy)
         quant_w(2)
         project(2, 0, T, nc.scalar.copy, aux[3])
-        cast_plane(1)
-        cast_plane(2)
+        cast_plane(1, nc.scalar.copy)
+        cast_plane(2, nc.scalar.copy)
         quant_w(3)
         project(3, 0, T, nc.scalar.copy, aux[2])
         corners(0, 0, BLOCKS, 1)

from contextlib import ExitStack

import concourse.mybir as mybir

K, T, N = 512, 512, 512
FLOPS = 2 * K * T * N

F32 = mybir.dt.float32
BF16 = mybir.dt.bfloat16
I32 = mybir.dt.int32
U32 = mybir.dt.uint32
U16 = mybir.dt.uint16
U8 = mybir.dt.uint8
FP8X4 = mybir.dt.float8_e4m3fn_x4
MULT = mybir.AluOpType.mult
ADD = mybir.AluOpType.add

P = 128
PACK = 4
BLOCKS = 4
SPARE = 16
PIECES = [(0, 44), (44, 88), (88, 128)]
PIECE_AT = [352, 0, 704]
DRAINS = [(0, 42), (42, 85), (85, 128)]


def tile_picked_wbilin_none_lo_kernel(tc, x_words, x_scales, w1, fx, fy, c00, c01, c10, c11, out_0, out_1, out_2):
    nc = tc.nc
    with ExitStack() as ctx:
        keep = ctx.enter_context(tc.tile_pool(name="keep", bufs=1))
        sums = ctx.enter_context(tc.psum_pool(name="sums", bufs=1))
        auxp = ctx.enter_context(tc.psum_pool(name="aux", bufs=1))
        aux = [auxp.tile([P, T], F32, name=f"aux{a}") for a in range(4)]

        lists = [keep.tile([P, T // 16], U16, name=f"list{i}") for i in range(4)]
        list_src = [c11, c10, c00, c01]
        xw = keep.tile([P, T], U32, name="xw", align_bytes=64)
        xs = keep.tile([P, T], U8, name="xs", align_bytes=64)
        w_stage = keep.tile([P, 1344], F32, name="w_stage")
        w_raw = [
            w_stage[:, at : at + 16 * (q1 - q0)].rearrange("p (j m) -> p j m", j=PACK)
            for (q0, q1), at in zip(PIECES, PIECE_AT)
        ]
        w_rows = w1.rearrange("(p j) m -> p j m", j=PACK)
        ax = keep.tile([P, 2, PACK], F32, name="ax")
        ay = keep.tile([P, 2, PACK], F32, name="ay")

        def load_w(a):
            q0, q1 = PIECES[a]
            nc.sync.dma_start(w_raw[a], w_rows[:, :, 4 * q0 : 4 * q1])

        nc.vector.memset(xs[:].bitcast(I32), 0)
        nc.sync.dma_start(ax[:, 1, :], fx[0].rearrange("(p j) -> p j", j=PACK))
        nc.sync.dma_start(ay[:, 1, :], fy[0].rearrange("(p j) -> p j", j=PACK))
        load_w(0)
        for q in range(4):
            nc.sync.dma_start(xs[32 * q : 32 * q + 4, :].bitcast(I32), x_scales[0, 4 * q : 4 * q + 4, :].bitcast(I32))
        nc.sync.dma_start(xw[:].bitcast(I32), x_words[0].rearrange("p n r -> p (n r)").bitcast(I32))
        for i in range(4):
            nc.sync.dma_start(lists[i][:], list_src[i])

        ident = keep.tile([P, P], F32, name="ident")
        ones = keep.tile([P, 32], F32, name="ones")
        column = keep.tile([P, 32], F32, name="column", align_bytes=64)
        row = keep.tile([P, 32], F32, name="row", align_bytes=64)
        nc.vector.memset(ones[:], 1.0)
        nc.vector.memset(ident[:], 0.0)
        nc.vector.tensor_tensor_scan(column[:], ones[:], ones[:], 0.0, MULT, ADD)
        nc.vector.transpose(row[:], column[:])
        for q in range(4):
            rows = slice(32 * q, 32 * q + 32)
            nc.vector.tensor_tensor(ident[rows, rows], column[rows, :], row[rows, :], mybir.AluOpType.is_equal)
        y = [keep.tile([P, T + SPARE if b == 0 else T], F32, name=f"y{b}") for b in range(BLOCKS)]
        nc.vector.memset(y[0][:, T:], 0.0)
        w_words = keep.tile([P, 2 * N], F32, name="w_words", align_bytes=64)
        term0 = keep.tile([P, T], F32, name="term0")
        term1 = keep.tile([P, T], F32, name="term1")
        term3 = keep.tile([P, P + T], F32, name="term3")
        nc.vector.memset(term3[:, 0:P], 0.0)
        term = [term0[:], term1[:], w_words[:, 0:T], term3[:, P:]]

        wt = [keep.tile([P, PACK], F32, name=f"wt{i}") for i in range(4)]
        nc.vector.tensor_tensor(wt[0][:], ax[:, 1, :], ay[:, 1, :], MULT)
        nc.vector.tensor_scalar(ax[:, 0, :], ax[:, 1, :], -1.0, 1.0, MULT, ADD)
        nc.vector.tensor_scalar(ay[:, 0, :], ay[:, 1, :], -1.0, 1.0, MULT, ADD)
        nc.vector.tensor_tensor(wt[1][:], ax[:, 0, :], ay[:, 1, :], MULT)
        nc.vector.tensor_tensor(wt[2][:], ax[:, 0, :], ay[:, 0, :], MULT)
        nc.vector.tensor_tensor(wt[3][:], ax[:, 1, :], ay[:, 0, :], MULT)
        cw = [keep.tile([P, T], F32, name=f"cw{i}") for i in range(4)]
        acc = [sums.tile([P, N], F32, name=f"acc{h}") for h in range(BLOCKS)]

        def spread(i, copy, bank):
            for j in range(PACK):
                nc.tensor.transpose(bank[:, j * P : (j + 1) * P], wt[i][:, j : j + 1].to_broadcast([P, P]), ident[:])
            copy(cw[i][:].rearrange("q (n j) -> q n j", j=PACK), bank[:].rearrange("q (j n) -> q n j", j=PACK))

        w_bf = w_words[:].bitcast(BF16)
        w_codes = [keep.tile([P, P], U32, name=f"w_codes{b}", align_bytes=64) for b in range(BLOCKS)]
        w_sc = [keep.tile([P, P], U8, name=f"w_sc{b}", align_bytes=64) for b in range(BLOCKS)]

        def cast_mixed(a, copy):
            q0, q1 = PIECES[a]
            copy(
                w_bf[:, 12 * q0 : 12 * q1].rearrange("p (q t j) -> p q j t", t=3, j=PACK),
                w_raw[a].rearrange("p j (q t) -> p q j t", t=PACK)[:, :, :, 0:3],
            )

        def cast_plane(a, copy):
            q0, q1 = PIECES[a]
            copy(
                w_bf[:, 1536 + 4 * q0 : 1536 + 4 * q1].rearrange("p (q j) -> p q j", j=PACK),
                w_raw[a].rearrange("p j (q t) -> p q j t", t=PACK)[:, :, :, 3],
            )

        def quant_w(b):
            nc.vector.quantize_mx(out=w_codes[b][:].bitcast(FP8X4), scales=w_sc[b][:], in_=w_bf[:, b * T : (b + 1) * T])

        def project(b, lo, hi, copy, bank):
            nc.tensor.matmul_mx(
                out=bank[:, 0 : hi - lo], lhsT=w_codes[b][:].bitcast(FP8X4), lhsT_scale=w_sc[b][:],
                rhs=xw[:, lo:hi].bitcast(FP8X4), rhs_scale=xs[:, lo:hi], start=True, stop=True,
            )
            copy(y[b][:, lo:hi], bank[:, 0 : hi - lo])

        st = [keep.tile([P, PACK, P], F32, name=f"st{h}") for h in range(BLOCKS)]

        def look_up(g, b, i, h0, h1):
            nc.vector.tensor_tensor(g, y[b][:].indirect(lists[i][:, h0 * 8 : h1 * 8]), cw[i][:, h0 * P : h1 * P], MULT)

        def gather(b, i, h0, h1):
            n = (h1 - h0) * P
            g = term[i][:, 0:n]
            if i == 0 and h0 == 0 and b in (1, 2):
                g = w_words[:, (b + 1) * 256 : (b + 2) * 256]
            look_up(g, b, i, h0, h1)
            for h in range(h0, h1):
                nc.tensor.matmul(
                    acc[h][:, b * P : (b + 1) * P], lhsT=g[:, (h - h0) * P : (h - h0 + 1) * P], rhs=ident[:],
                    is_transpose=True, start=(i == 0), stop=(i == 3),
                )

        def drain(b, h):
            if b < 3:
                q0, q1 = DRAINS[b]
                nc.scalar.copy(st[h][:, 0:3, q0:q1], acc[h][:, 3 * q0 : 3 * q1].rearrange("v (q t) -> v t q", t=3))
            else:
                nc.scalar.copy(st[h][:, 3, :], acc[h][:, 3 * P :])

        def turn_back(h, bank, planes):
            for t in range(planes):
                nc.tensor.transpose(bank[:, t * P : (t + 1) * P], st[h][:, t, :], ident[:])

        words = keep.tile([P, T], U32, name="words", align_bytes=64)
        scales = keep.tile([P, T], U8, name="scales", align_bytes=64)
        out_rows = out_0.rearrange("(p t) v -> p t v", t=PACK)
        out_words = out_1[0].rearrange("p n r -> p (n r)").bitcast(I32)
        o = [keep.tile([P, PACK, P], F32, name=f"o{h}") for h in range(BLOCKS)]

        def store_f32(h, bank, planes):
            nc.scalar.copy(o[h][:, 0:planes, :], bank[:, 0 : planes * P].rearrange("p (t v) -> p t v", t=planes))
            nc.sync.dma_start(out_rows[:, 0:planes, h * P : (h + 1) * P], o[h][:, 0:planes, :])

        r = keep.tile([P, T * PACK], BF16, name="r", align_bytes=64)

        def rounded(h):
            return r[:, h * T : (h + 1) * T].rearrange("p (v t) -> p v t", t=PACK)

        def round_bf16(h, bank, planes):
            nc.scalar.copy(rounded(h)[:, :, 0:planes], bank[:, 0 : planes * P].rearrange("p (t v) -> p v t", t=planes))

        def quant_out(h0, h1):
            cols = slice(h0 * P, h1 * P)
            nc.vector.quantize_mx(out=words[:, cols].bitcast(FP8X4), scales=scales[:, cols], in_=r[:, h0 * T : h1 * T])
            nc.sync.dma_start(out_words[:, cols], words[:, cols].bitcast(I32))

        cast_mixed(0, nc.vector.tensor_copy)
        cast_plane(0, nc.vector.tensor_copy)
        load_w(1)
        load_w(2)
        quant_w(0)
        spread(0, nc.scalar.copy, aux[2])
        project(0, 0, 256, nc.vector.tensor_copy, aux[0])
        project(0, 256, T, nc.scalar.copy, aux[1])
        spread(1, nc.scalar.copy, aux[3])
        cast_mixed(1, nc.scalar.copy)
        spread(2, nc.scalar.copy, aux[0])
        spread(3, nc.scalar.copy, aux[1])

        def corners(b, h0, h1, first=0):
            for i in range(first, 4):
                gather(b, i, h0, h1)
            for h in range(h0, h1):
                drain(b, h)

        gather(0, 0, 0, BLOCKS)
        quant_w(1)
        project(1, 0, T, nc.scalar.copy, aux[2])
        cast_mixed(2, nc.scalar.copy)
        quant_w(2)
        project(2, 0, T, nc.scalar.copy, aux[3])
        cast_plane(1, nc.scalar.copy)
        cast_plane(2, nc.scalar.copy)
        quant_w(3)
        project(3, 0, T, nc.scalar.copy, aux[2])
        corners(0, 0, BLOCKS, 1)
        corners(1, 0, 2)
        corners(2, 0, 2)
        corners(3, 0, 2)
        turn_back(0, aux[0], 4)
        turn_back(1, aux[1], 4)
        for h in range(2):
            round_bf16(h, aux[h], 4)
            store_f32(h, aux[h], 4)
        corners(1, 2, 4)
        corners(2, 2, 4)
        turn_back(3, aux[2], 3)
        corners(3, 2, 3)
        turn_back(2, aux[3], 4)
        store_f32(3, aux[2], 3)
        round_bf16(3, aux[2], 2)
        round_bf16(2, aux[3], 4)
        store_f32(2, aux[3], 4)

        pair_sum = keep.tile([P, P], F32, name="pair_sum")
        for i in range(3):
            look_up(term[i][:, 0:P], 3, i, 3, 4)
        nc.vector.tensor_tensor(pair_sum[:], term[0][:, 0:P], term[1][:, 0:P], ADD)
        quant_out(0, 2)
        nc.vector.tensor_tensor(o[3][:, 3, :], pair_sum[:], term[2][:, 0:P], ADD)
        look_up(term[3][:, 0:P], 3, 3, 3, 4)
        nc.vector.tensor_tensor(
            rounded(3)[:, :, 2:4],
            o[3][:, 2:4, :].rearrange("p t v -> p v t"),
            term3[:, 0 : 2 * P].rearrange("p (t v) -> p v t", t=2),
            ADD,
        )
        final = keep.tile([P, P], F32, name="final")
        nc.vector.tensor_tensor(final[:], o[3][:, 3, :], term[3][:, 0:P], ADD)
        nc.scalar.dma_start(out_rows[:, 3, 3 * P :], final[:])
        quant_out(2, 4)
        for q in range(4):
            eng = nc.sync if q < 2 else nc.scalar
            eng.dma_start(out_2[0, 4 * q : 4 * q + 4, :].bitcast(I32), scales[32 * q : 32 * q + 4, :].bitcast(I32))
